import numpy as np
import ml_dtypes


def mxq(x, axis, fmt="e4m3"):
    dtype, down = {"e4m3": (ml_dtypes.float8_e4m3fn, 7), "e5m2": (ml_dtypes.float8_e5m2, 14)}[fmt]
    v = np.moveaxis(np.asarray(x, np.float32).astype(ml_dtypes.bfloat16).astype(np.float64), axis, -1)
    blocks = v.reshape(v.shape[:-1] + (-1, 32))
    amax = np.abs(blocks).max(-1, keepdims=True)
    byte = np.maximum(np.where(amax > 0, np.frexp(amax)[1] - 1 + 127, 0) - down, 1)
    scale = np.exp2(byte - 127.0)
    codes = (blocks / scale).astype(np.float32).astype(dtype).astype(np.float64)
    return np.moveaxis((codes * scale).reshape(v.shape), -1, axis)


WIDE = False


def mx_kscale(k):
    if not WIDE:
        return np.ones(k)
    levels = np.array([10, -10, 5, -5, 0])
    if k % 512:
        return np.exp2(np.random.permutation(np.resize(levels, k // 32))).repeat(32)
    a = np.empty((k // 512, 16))
    for p in range(k // 512):
        a[p, :8] = np.random.permutation(np.resize(levels, 8))
        for g in range(8):
            far = levels[np.abs(levels - a[p, g]) >= 10]
            a[p, g + 8] = far[np.random.randint(len(far))]
    return np.exp2(a.ravel()).repeat(32)


BF16 = ml_dtypes.bfloat16


def bf(x):
    return np.asarray(x, np.float32).astype(BF16)


def f64(x):
    return np.asarray(x).astype(np.float64)

E4M3FN = np.array([(-1.0 if i & 128 else 1.0) * ((1.0 + (i & 7) / 8.0) * 2.0 ** (((i >> 3) & 15) - 7) if i & 120 else (i & 7) * 2.0 ** -9) for i in range(256)])


def e4m3fn_bytes(y):
    return np.clip(np.asarray(y, np.float64), -448.0, 448.0).astype(np.float32).astype(ml_dtypes.float8_e4m3fn).view(np.uint8)


def e4m3fn_values(b):
    return E4M3FN[b]


Q, T, K = 512, 4096, 2048


def setup_inputs():
    s = mx_kscale(K)
    length = np.random.uniform(0.5, 1.5, (T, 1))
    keys = np.random.standard_normal((T, K)) * length * s
    scale = (np.abs(keys).max(axis=1, keepdims=True) / 448).astype(np.float32)
    return {"query": bf(np.random.standard_normal((Q, K)) / np.sqrt(K) / s),
            "keys_bytes": e4m3fn_bytes(keys / f64(scale)),
            "keys_scale": scale,
            "age": bf(np.random.exponential(2.0, T)),
            "rate": bf(0.2 + 0.3 * np.abs(np.random.standard_normal(Q)))}


def reference(query, keys_bytes, keys_scale, age, rate):
    keys = e4m3fn_values(keys_bytes) * np.repeat(f64(keys_scale), K, axis=1)
    match = mxq(f64(query), 1, "e4m3") @ mxq(keys, 1, "e4m3").T
    staleness = np.log(1.0 + f64(age))
    return match - f64(rate)[:, None] * staleness[None, :]

@@ -1,0 +1,254 @@
+from contextlib import ExitStack
+
+import concourse.mybir as mybir
+from concourse.masks import make_identity
+
+Q, T, K = 512, 4096, 2048
+FLOPS = 2 * Q * T * K
+
+F32 = mybir.dt.float32
+BF16 = mybir.dt.bfloat16
+U32 = mybir.dt.uint32
+U8 = mybir.dt.uint8
+FP8 = mybir.dt.float8_e4m3fn
+FP8X4 = mybir.dt.float8_e4m3fn_x4
+MULT = mybir.AluOpType.mult
+ADD = mybir.AluOpType.add
+COPY = mybir.ActivationFunctionType.Copy
+LN = mybir.ActivationFunctionType.Ln
+ENGINES = {mybir.EngineType.PE, mybir.EngineType.DVE, mybir.EngineType.Activation, mybir.EngineType.SP}
+
+P = 128
+G = 4
+NT = 4
+CH = NT * P
+CHUNKS = T // CH
+M = Q // P
+
+
+def tile_aged_key_retrieval_d3_kernel(tc, query, keys_bytes, keys_scale, age, rate, out):
+    nc = tc.nc
+    with ExitStack() as ctx:
+        const = ctx.enter_context(tc.tile_pool(name="const", bufs=1))
+        raw_pool = ctx.enter_context(tc.tile_pool(name="raw", bufs=CHUNKS))
+        wide_pool = ctx.enter_context(tc.tile_pool(name="wide", bufs=3))
+        group_pool = ctx.enter_context(tc.tile_pool(name="group", bufs=2))
+        code_pool = ctx.enter_context(tc.tile_pool(name="code", bufs=2))
+        out_pool = ctx.enter_context(tc.tile_pool(name="outs", bufs=6))
+        turn_psum = ctx.enter_context(tc.psum_pool(name="turn", bufs=6))
+        acc_psum = ctx.enter_context(tc.psum_pool(name="acc", bufs=2))
+
+        ident = const.tile([P, P], F32, name="ident")
+        key_scale0 = const.tile([P, NT], F32, name="key_scale0")
+        key_scale1 = const.tile([P, CHUNKS - 1, NT], F32, name="key_scale1")
+        age_sb = const.tile([P, T // P], BF16, name="age_sb")
+        stale_sb = const.tile([P, T // P], F32, name="stale_sb")
+        rate_sb = const.tile([P, M], BF16, name="rate_sb")
+        neg_rate = const.tile([P, M], F32, name="neg_rate")
+        stale = const.tile([P, T], F32, name="stale")
+        query_sb = const.tile([P, M, K], BF16, name="query_sb")
+        q_codes = const.tile([P, M, G, P], U32, name="q_codes", align_bytes=64)
+        q_scales = const.tile([P, M, G, P], U8, name="q_scales", align_bytes=64)
+
+        scale_view = keys_scale.rearrange("(c p i) o -> p c (i o)", p=P, i=NT)
+        key_view = keys_bytes.rearrange("(c p i) k -> c p i k", p=P, i=NT)
+        query_view = query.rearrange("(p m) k -> p m k", m=M)
+        out_view = out.rearrange("(p m) n -> p m n", m=M)
+        park = out[Q - 1 : Q, :]
+
+        raws, nats, splits, groups, codes, banks, accs = {}, {}, {}, {}, {}, {}, {}
+
+        def scale_col(c, i):
+            if c == 0:
+                return key_scale0[:, i : i + 1]
+            return key_scale1[:, c - 1, i : i + 1]
+
+        def load(c, parts):
+            raws[c] = raw_pool.tile([P, NT, K], U8, name="raw")
+            n = NT // parts
+            for i in range(parts):
+                nc.sync.dma_start(out=raws[c][:, i * n : (i + 1) * n, :], in_=key_view[c][:, i * n : (i + 1) * n, :])
+
+        def widen_s(c, i):
+            if i == 0:
+                nats[c] = wide_pool.tile([P, K + 512], BF16, name="nat")
+            b = K if i == 0 else 512
+            nc.scalar.activation(
+                out=nats[c][:, K * i : K * i + b], in_=raws[c][:, i, :b].bitcast(FP8), func=COPY, scale=scale_col(c, i))
+
+        def widen_v(c, i):
+            if i == 1:
+                splits[c] = wide_pool.tile([P, NT - 1, 2, 512, 2], BF16, name="split")
+            w0 = P if i == 1 else 0
+            nc.vector.tensor_scalar(
+                out=splits[c][:, i - 1, :, w0:, :].rearrange("p u w e -> p w u e"),
+                in0=raws[c][:, i, 4 * w0 :].bitcast(FP8).rearrange("p (w u e) -> p w u e", u=2, e=2),
+                scalar1=scale_col(c, i), scalar2=None, op0=MULT)
+
+        def words(c, i, g, u):
+            if i == 0 or (i == 1 and g == 0):
+                w = nats[c][:, K * i : K * i + (K if i == 0 else 512)].bitcast(F32)
+                return w[:, 256 * g + u : 256 * (g + 1) : 2]
+            w = splits[c][:, i - 1, u].rearrange("p w e -> p (w e)").bitcast(F32)
+            return w[:, P * g : P * (g + 1)]
+
+        def turn(c, g, h):
+            bank = turn_psum.tile([P, 2, 2, P], F32, name="bank")
+            banks[c, g, h] = bank
+            for j in range(2):
+                for u in range(2):
+                    nc.tensor.transpose(bank[:, u, j, :], words(c, 2 * h + j, g, u), ident[:])
+
+        def group(c, g, h):
+            if g == 0 and h == 0:
+                groups[c] = group_pool.tile([P, G, CH, 4], BF16, name="grp", align_bytes=64)
+            dst = groups[c][:, g, 256 * h : 256 * (h + 1), :].bitcast(F32)
+            nc.scalar.copy(out=dst, in_=banks[c, g, h][:].rearrange("p u j r -> p (j r) u"))
+
+        def turn_q(m, h):
+            bank = turn_psum.tile([P, 2, 2, P], F32, name="bank")
+            banks["q", m, h] = bank
+            w = query_sb[:, m, :].bitcast(F32)
+            for j in range(2):
+                for u in range(2):
+                    g = 2 * h + j
+                    nc.tensor.transpose(bank[:, j, u, :], w[:, 256 * g + u : 256 * (g + 1) : 2], ident[:])
+
+        def group_q(m, h):
+            if m == 0 and h == 0:
+                groups["q"] = group_pool.tile([P, G, CH, 4], BF16, name="grp", align_bytes=64)
+            copy = nc.vector.tensor_copy if h else nc.scalar.copy
+            dst = groups["q"][:, m, 256 * h : 256 * (h + 1), :].bitcast(F32).rearrange("p (j r) u -> p j r u", j=2)
+            copy(out=dst, in_=banks["q", m, h][:].rearrange("p j u r -> p j r u"))
+
+        def quant_q(m):
+            nc.vector.quantize_mx(
+                out=q_codes[:, m].rearrange("p g r -> p (g r)").bitcast(FP8X4),
+                scales=q_scales[:, m].rearrange("p g r -> p (g r)"),
+                in_=groups["q"][:, m].rearrange("p n t -> p (n t)"))
+
+        def quant(c, g):
+            if g == 0:
+                kc = code_pool.tile([P, G, CH], U32, name="kc", align_bytes=64)
+                ks = code_pool.tile([P, G, CH], U8, name="ks", align_bytes=64)
+                codes[c] = (kc, ks)
+            kc, ks = codes[c]
+            nc.vector.quantize_mx(
+                out=kc[:, g, :].bitcast(FP8X4), scales=ks[:, g, :], in_=groups[c][:, g].rearrange("p n t -> p (n t)"))
+
+        def multiply(c, m):
+            kc, ks = codes[c]
+            acc = acc_psum.tile([P, CH], F32, name="acc")
+            accs[c, m] = acc
+            for g in range(G):
+                nc.tensor.matmul_mx(
+                    out=acc[:], lhsT=q_codes[:, m, g, :].bitcast(FP8X4), lhsT_scale=q_scales[:, m, g, :],
+                    rhs=kc[:, g, :].bitcast(FP8X4), rhs_scale=ks[:, g, :],
+                    start=(g == 0), stop=(g == G - 1))
+
+        def finish(c, m):
+            res = out_pool.tile([P, CH], F32, name="res")
+            nc.vector.scalar_tensor_tensor(
+                out=res[:].rearrange("p (r i) -> p r i", i=NT),
+                in0=stale[:, CH * c : CH * (c + 1)].rearrange("p (r i) -> p r i", i=NT),
+                scalar=neg_rate[:, m : m + 1],
+                in1=accs[c, m][:].rearrange("p (i r) -> p r i", i=NT),
+                op0=MULT, op1=ADD)
+            nc.sync.dma_start(out=out_view[:, m, CH * c : CH * (c + 1)], in_=res[:])
+
+        run = {"Ws": widen_s, "Wv": widen_v, "T": turn, "E": group, "Q": quant, "M": multiply, "O": finish,
+               "Tq": turn_q, "Eq": group_q, "Qq": quant_q}
+
+        def needs(op):
+            k, a = op[0], op[1:]
+            if k == "T":
+                return [(("Ws" if 4 * i + a[1] < 5 else "Wv"), a[0], i) for i in (2 * a[2], 2 * a[2] + 1)]
+            if k == "E":
+                return [("T",) + a]
+            if k == "Q":
+                return [("E",) + a + (h,) for h in range(2)]
+            if k == "M":
+                return [("Q", a[0], g) for g in range(G)] + [("Qq", a[1])]
+            if k == "O":
+                return [("M",) + a]
+            if k == "Eq":
+                return [("Tq",) + a]
+            if k == "Qq":
+                return [("Eq",) + a + (h,) for h in range(2)]
+            return []
+
+        def Ts(c):
+            return [("T", c, g, h) for g in range(G) for h in range(2)]
+
+        def Es(c):
+            return [("E", c, g, h) for g in range(G) for h in range(2)]
+
+        def Ms(c):
+            return [("M", c, m) for m in range(M)]
+
+        pe = Ts(0) + [("Tq", m, h) for m in range(M) for h in range(2)] + Ms(0) + Ts(1)
+        act = [("Ws", 0, 0), ("Ws", 0, 1), ("Ws", 1, 0)] + Es(0) + [("Eq", m, 0) for m in range(M)]
+        act += [("Ws", 1, 1), ("Ws", 2, 0), ("Ws", 2, 1)] + Es(1) + [("Ws", 3, 0)]
+        dve = [("Wv", 0, i) for i in (1, 2, 3)] + [("Wv", 1, i) for i in (1, 2, 3)]
+        dve += [("Q", 0, 0), ("Q", 0, 1), ("Eq", 0, 1), ("Q", 0, 2), ("Eq", 1, 1), ("Q", 0, 3), ("Eq", 2, 1), ("Qq", 0), ("Eq", 3, 1),
+                ("Qq", 1), ("Qq", 2), ("O", 0, 0), ("Qq", 3), ("O", 0, 1), ("Wv", 2, 1), ("O", 0, 2), ("O", 0, 3), ("Wv", 2, 2), ("Wv", 2, 3),
+                ("Q", 1, 0), ("Q", 1, 1), ("Wv", 3, 1), ("Q", 1, 2), ("Q", 1, 3), ("Wv", 3, 2)]
+        for c in range(1, CHUNKS):
+            n, w = c + 1, c + 2
+            if n < CHUNKS:
+                pe += Ts(n)
+                act += Es(n)
+            pe += Ms(c)
+            if w < CHUNKS:
+                act += [("Ws", w, 1)]
+            if w + 1 < CHUNKS:
+                act += [("Ws", w + 1, 0)]
+            first = [("Wv", w, 1), ("Q", n, 0), ("Wv", w, 2), ("Q", n, 1)] if c > 1 else [("Q", n, 0), ("Q", n, 1)]
+            rest = [("O", c, 0), ("Q", n, 2), ("O", c, 1), ("Q", n, 3), ("O", c, 2), ("Wv", w, 3), ("O", c, 3)]
+            dve += [op for op in first + rest if op[1] < CHUNKS]
+
+        with tc.manual_schedule(engines=ENGINES):
+            nc.scalar.dma_start(out=key_scale0[:], in_=scale_view[:, 0, :])
+            nc.scalar.dma_start(out=age_sb[:], in_=age.rearrange("(p i) -> p i", p=P))
+            nc.scalar.dma_start(out=key_scale1[:], in_=scale_view[:, 1:, :])
+            nc.scalar.dma_start(out=rate_sb[:], in_=rate.rearrange("(p m) -> p m", m=M))
+            load(0, NT)
+            make_identity(nc, ident[:])
+            load(1, 2)
+            for m in range(M):
+                nc.sync.dma_start(out=query_sb[:, m, :], in_=query_view[:, m, :])
+            nc.scalar.activation(out=stale_sb[:], in_=age_sb[:], func=LN, bias=1.0)
+            nc.scalar.dma_start(out=park.rearrange("o (p i) -> p (o i)", p=P), in_=stale_sb[:])
+            nc.gpsimd.tensor_scalar(out=neg_rate[:], in0=rate_sb[:], scalar1=-1.0, scalar2=None, op0=MULT)
+            load(2, 2)
+            for c in range(CHUNKS):
+                nc.sync.dma_start(out=stale[:, CH * c : CH * (c + 1)],
+                                  in_=park[0, CH * c : CH * (c + 1)].partition_broadcast(P))
+                if c + 3 < CHUNKS:
+                    load(c + 3, 2)
+
+            queues = [pe, act, dve]
+            turns = [op for op in pe if op[0] in ("T", "Tq")]
+            mults = [op for op in pe if op[0] == "M"]
+            after = {}
+            for a, b in zip(turns, turns[6:]):
+                after[b] = ("E" + a[0][1:],) + a[1:]
+            for a, b in zip(mults, mults[2:]):
+                after[b] = ("O",) + a[1:]
+            for c in range(CHUNKS):
+                if c >= 3:
+                    after["Ws", c, 0] = after["Wv", c, 1] = ("T", c - 3, 3, 1)
+                if c >= 2:
+                    after["Q", c, 0] = ("M", c - 2, 3)
+                    after["E", c, 0, 0] = ("Qq", 3) if c == 2 else ("Q", c - 2, 3)
+            after["E", 1, 0, 0] = ("Q", 0, 3)
+            heads = [0, 0, 0]
+            done = set()
+            for lap in range(500):
+                for e in range(3):
+                    while heads[e] < len(queues[e]) and all(
+                        d in done for d in needs(queues[e][heads[e]]) + [after[op] for op in [queues[e][heads[e]]] if op in after]):
+                        op = queues[e][heads[e]]
+                        run[op[0]](*op[1:])
+                        done.add(op)
+                        heads[e] += 1

@@ -30,8 +30,8 @@ def tile_aged_key_retrieval_d3_kernel(tc, query, keys_bytes, keys_scale, age, ra
     nc = tc.nc
     with ExitStack() as ctx:
         const = ctx.enter_context(tc.tile_pool(name="const", bufs=1))
-        raw_pool = ctx.enter_context(tc.tile_pool(name="raw", bufs=CHUNKS))
-        wide_pool = ctx.enter_context(tc.tile_pool(name="wide", bufs=3))
+        raw_pool = ctx.enter_context(tc.tile_pool(name="raw", bufs=7))
+        wide_pool = ctx.enter_context(tc.tile_pool(name="wide", bufs=4))
         group_pool = ctx.enter_context(tc.tile_pool(name="group", bufs=2))
         code_pool = ctx.enter_context(tc.tile_pool(name="code", bufs=2))
         out_pool = ctx.enter_context(tc.tile_pool(name="outs", bufs=6))
@@ -117,9 +117,8 @@ def tile_aged_key_retrieval_d3_kernel(tc, query, keys_bytes, keys_scale, age, ra
         def group_q(m, h):
             if m == 0 and h == 0:
                 groups["q"] = group_pool.tile([P, G, CH, 4], BF16, name="grp", align_bytes=64)
-            copy = nc.vector.tensor_copy if h else nc.scalar.copy
             dst = groups["q"][:, m, 256 * h : 256 * (h + 1), :].bitcast(F32).rearrange("p (j r) u -> p j r u", j=2)
-            copy(out=dst, in_=banks["q", m, h][:].rearrange("p j u r -> p j r u"))
+            nc.scalar.copy(out=dst, in_=banks["q", m, h][:].rearrange("p j u r -> p j r u"))
 
         def quant_q(m):
             nc.vector.quantize_mx(
@@ -186,26 +185,19 @@ def tile_aged_key_retrieval_d3_kernel(tc, query, keys_bytes, keys_scale, age, ra
         def Ms(c):
             return [("M", c, m) for m in range(M)]
 
-        pe = Ts(0) + [("Tq", m, h) for m in range(M) for h in range(2)] + Ms(0) + Ts(1)
-        act = [("Ws", 0, 0), ("Ws", 0, 1), ("Ws", 1, 0)] + Es(0) + [("Eq", m, 0) for m in range(M)]
-        act += [("Ws", 1, 1), ("Ws", 2, 0), ("Ws", 2, 1)] + Es(1) + [("Ws", 3, 0)]
-        dve = [("Wv", 0, i) for i in (1, 2, 3)] + [("Wv", 1, i) for i in (1, 2, 3)]
-        dve += [("Q", 0, 0), ("Q", 0, 1), ("Eq", 0, 1), ("Q", 0, 2), ("Eq", 1, 1), ("Q", 0, 3), ("Eq", 2, 1), ("Qq", 0), ("Eq", 3, 1),
-                ("Qq", 1), ("Qq", 2), ("O", 0, 0), ("Qq", 3), ("O", 0, 1), ("Wv", 2, 1), ("O", 0, 2), ("O", 0, 3), ("Wv", 2, 2), ("Wv", 2, 3),
-                ("Q", 1, 0), ("Q", 1, 1), ("Wv", 3, 1), ("Q", 1, 2), ("Q", 1, 3), ("Wv", 3, 2)]
-        for c in range(1, CHUNKS):
-            n, w = c + 1, c + 2
-            if n < CHUNKS:
-                pe += Ts(n)
-                act += Es(n)
-            pe += Ms(c)
-            if w < CHUNKS:
-                act += [("Ws", w, 1)]
-            if w + 1 < CHUNKS:
-                act += [("Ws", w + 1, 0)]
-            first = [("Wv", w, 1), ("Q", n, 0), ("Wv", w, 2), ("Q", n, 1)] if c > 1 else [("Q", n, 0), ("Q", n, 1)]
-            rest = [("O", c, 0), ("Q", n, 2), ("O", c, 1), ("Q", n, 3), ("O", c, 2), ("Wv", w, 3), ("O", c, 3)]
-            dve += [op for op in first + rest if op[1] < CHUNKS]
+        pe = Ts(0) + [("Tq", m, h) for m in range(M) for h in range(2)]
+        act = [("Ws", c, i) for c in (0, 1) for i in (0, 1)] + Es(0) + [("Eq", m, h) for m in range(M) for h in range(2)]
+        act += [("Ws", 2, 0), ("Ws", 2, 1)]
+        dve = [("Wv", c, i) for c in (0, 1) for i in (1, 2, 3)]
+        dve += [("Q", 0, 0), ("Q", 0, 1), ("Q", 0, 2), ("Wv", 2, 1), ("Q", 0, 3), ("Wv", 2, 2), ("Qq", 0), ("Qq", 1), ("Qq", 2), ("Wv", 2, 3), ("Qq", 3)]
+        for c in range(CHUNKS):
+            n, w = c + 1, c + 3
+            t, m = (Ts(n) if n < CHUNKS else []), Ms(c)
+            pe += t[:4] + m[:2] + t[4:] + m[2:]
+            act += [op for op in Es(n) + [("Ws", w, 0), ("Ws", w, 1)] if op[1] < CHUNKS]
+            dve += [op for op in [
+                ("O", c, 0), ("O", c, 1), ("Q", n, 0), ("Q", n, 1), ("Wv", w, 1),
+                ("O", c, 2), ("Q", n, 2), ("O", c, 3), ("Q", n, 3), ("Wv", w, 2), ("Wv", w, 3)] if op[1] < CHUNKS]
 
         with tc.manual_schedule(engines=ENGINES):
             nc.scalar.dma_start(out=key_scale0[:], in_=scale_view[:, 0, :])
@@ -236,8 +228,8 @@ def tile_aged_key_retrieval_d3_kernel(tc, query, keys_bytes, keys_scale, age, ra
             for a, b in zip(mults, mults[2:]):
                 after[b] = ("O",) + a[1:]
             for c in range(CHUNKS):
-                if c >= 3:
-                    after["Ws", c, 0] = after["Wv", c, 1] = ("T", c - 3, 3, 1)
+                if c >= 4:
+                    after["Ws", c, 0] = after["Wv", c, 1] = ("T", c - 4, 3, 1)
                 if c >= 2:
                     after["Q", c, 0] = ("M", c - 2, 3)
                     after["E", c, 0, 0] = ("Qq", 3) if c == 2 else ("Q", c - 2, 3)

@@ -16,231 +16,259 @@ MULT = mybir.AluOpType.mult
 ADD = mybir.AluOpType.add
 COPY = mybir.ActivationFunctionType.Copy
 LN = mybir.ActivationFunctionType.Ln
-ENGINES = {mybir.EngineType.PE, mybir.EngineType.DVE, mybir.EngineType.Activation, mybir.EngineType.SP}
 
 P = 128
-G = 4
-NT = 4
-CH = NT * P
-CHUNKS = T // CH
+PASS = 512
+G = K // PASS
+PAIRS = PASS // 2
+CHUNK = 512
+NT = CHUNK // P
+NC = T // CHUNK
 M = Q // P
+
+SCALAR_WIDTHS = (K, PASS)
+
+RAW_BUFS = 5
+WIDE_BUFS = 4
+TURN_BANKS = 5
+SUM_BANKS = 3
+WARM_UP_HEAD = 14
 
 
 def tile_aged_key_retrieval_d3_kernel(tc, query, keys_bytes, keys_scale, age, rate, out):
     nc = tc.nc
     with ExitStack() as ctx:
         const = ctx.enter_context(tc.tile_pool(name="const", bufs=1))
-        raw_pool = ctx.enter_context(tc.tile_pool(name="raw", bufs=7))
-        wide_pool = ctx.enter_context(tc.tile_pool(name="wide", bufs=4))
-        group_pool = ctx.enter_context(tc.tile_pool(name="group", bufs=2))
+        raw_pool = ctx.enter_context(tc.tile_pool(name="raw", bufs=RAW_BUFS))
+        wide_pool = ctx.enter_context(tc.tile_pool(name="wide", bufs=WIDE_BUFS))
+        turned_pool = ctx.enter_context(tc.tile_pool(name="turned", bufs=2))
         code_pool = ctx.enter_context(tc.tile_pool(name="code", bufs=2))
-        out_pool = ctx.enter_context(tc.tile_pool(name="outs", bufs=6))
-        turn_psum = ctx.enter_context(tc.psum_pool(name="turn", bufs=6))
-        acc_psum = ctx.enter_context(tc.psum_pool(name="acc", bufs=2))
+        result_pool = ctx.enter_context(tc.tile_pool(name="result", bufs=6))
+        turn_psum = ctx.enter_context(tc.psum_pool(name="turn", bufs=TURN_BANKS))
+        sum_psum = ctx.enter_context(tc.psum_pool(name="sum", bufs=SUM_BANKS))
 
         ident = const.tile([P, P], F32, name="ident")
-        key_scale0 = const.tile([P, NT], F32, name="key_scale0")
-        key_scale1 = const.tile([P, CHUNKS - 1, NT], F32, name="key_scale1")
+        zeros = const.tile([P, CHUNK], BF16, name="zeros")
+        scale_first = const.tile([P, NT], F32, name="scale_first")
+        scale_rest = const.tile([P, NC - 1, NT], F32, name="scale_rest")
         age_sb = const.tile([P, T // P], BF16, name="age_sb")
         stale_sb = const.tile([P, T // P], F32, name="stale_sb")
+        stale = const.tile([P, T], F32, name="stale")
         rate_sb = const.tile([P, M], BF16, name="rate_sb")
         neg_rate = const.tile([P, M], F32, name="neg_rate")
-        stale = const.tile([P, T], F32, name="stale")
         query_sb = const.tile([P, M, K], BF16, name="query_sb")
         q_codes = const.tile([P, M, G, P], U32, name="q_codes", align_bytes=64)
         q_scales = const.tile([P, M, G, P], U8, name="q_scales", align_bytes=64)
 
-        scale_view = keys_scale.rearrange("(c p i) o -> p c (i o)", p=P, i=NT)
         key_view = keys_bytes.rearrange("(c p i) k -> c p i k", p=P, i=NT)
+        scale_view = keys_scale.rearrange("(c p i) o -> p c (i o)", p=P, i=NT)
         query_view = query.rearrange("(p m) k -> p m k", m=M)
         out_view = out.rearrange("(p m) n -> p m n", m=M)
         park = out[Q - 1 : Q, :]
 
-        raws, nats, splits, groups, codes, banks, accs = {}, {}, {}, {}, {}, {}, {}
+        raw, natural, split, turned, codes, banks, sums = {}, {}, {}, {}, {}, {}, {}
+
+        def load_keys(c, parts):
+            raw[c] = raw_pool.tile([P, NT, K], U8, name="raw_keys")
+            n = NT // parts
+            for i in range(0, NT, n):
+                nc.sync.dma_start(out=raw[c][:, i : i + n, :], in_=key_view[c][:, i : i + n, :])
+
+        def load_stale(c):
+            cols = slice(CHUNK * c, CHUNK * (c + 1))
+            nc.sync.dma_start(out=stale[:, cols], in_=park[0, cols].partition_broadcast(P))
 
         def scale_col(c, i):
-            if c == 0:
-                return key_scale0[:, i : i + 1]
-            return key_scale1[:, c - 1, i : i + 1]
+            return scale_first[:, i : i + 1] if c == 0 else scale_rest[:, c - 1, i : i + 1]
 
-        def load(c, parts):
-            raws[c] = raw_pool.tile([P, NT, K], U8, name="raw")
-            n = NT // parts
-            for i in range(parts):
-                nc.sync.dma_start(out=raws[c][:, i * n : (i + 1) * n, :], in_=key_view[c][:, i * n : (i + 1) * n, :])
 
-        def widen_s(c, i):
-            if i == 0:
-                nats[c] = wide_pool.tile([P, K + 512], BF16, name="nat")
-            b = K if i == 0 else 512
-            nc.scalar.activation(
-                out=nats[c][:, K * i : K * i + b], in_=raws[c][:, i, :b].bitcast(FP8), func=COPY, scale=scale_col(c, i))
+        def widen_scalar(c):
+            natural[c] = wide_pool.tile([P, sum(SCALAR_WIDTHS)], BF16, name="natural")
+            for i, width in enumerate(SCALAR_WIDTHS):
+                nc.scalar.activation(
+                    out=natural[c][:, K * i : K * i + width],
+                    in_=raw[c][:, i, :width].bitcast(FP8),
+                    func=COPY,
+                    scale=scale_col(c, i),
+                )
 
-        def widen_v(c, i):
+        def widen_vector(c, i):
             if i == 1:
-                splits[c] = wide_pool.tile([P, NT - 1, 2, 512, 2], BF16, name="split")
-            w0 = P if i == 1 else 0
+                split[c] = wide_pool.tile([P, NT - 1, 2, K // 4, 2], BF16, name="split")
+            k0 = SCALAR_WIDTHS[i] if i < len(SCALAR_WIDTHS) else 0
             nc.vector.tensor_scalar(
-                out=splits[c][:, i - 1, :, w0:, :].rearrange("p u w e -> p w u e"),
-                in0=raws[c][:, i, 4 * w0 :].bitcast(FP8).rearrange("p (w u e) -> p w u e", u=2, e=2),
-                scalar1=scale_col(c, i), scalar2=None, op0=MULT)
+                out=split[c][:, i - 1, :, k0 // 4 :, :].rearrange("p u w e -> p w u e"),
+                in0=raw[c][:, i, k0:].bitcast(FP8).rearrange("p (w u e) -> p w u e", u=2, e=2),
+                scalar1=scale_col(c, i),
+                scalar2=None,
+                op0=MULT,
+            )
 
-        def words(c, i, g, u):
-            if i == 0 or (i == 1 and g == 0):
-                w = nats[c][:, K * i : K * i + (K if i == 0 else 512)].bitcast(F32)
-                return w[:, 256 * g + u : 256 * (g + 1) : 2]
-            w = splits[c][:, i - 1, u].rearrange("p w e -> p (w e)").bitcast(F32)
-            return w[:, P * g : P * (g + 1)]
 
-        def turn(c, g, h):
+        def natural_pairs(row, g, u):
+            return row.bitcast(F32)[:, PAIRS * g + u : PAIRS * (g + 1) : 2]
+
+        def key_pairs(c, i, g, u):
+            if i < len(SCALAR_WIDTHS) and PASS * g < SCALAR_WIDTHS[i]:
+                return natural_pairs(natural[c][:, K * i : K * i + SCALAR_WIDTHS[i]], g, u)
+            half = split[c][:, i - 1, u].rearrange("p w e -> p (w e)").bitcast(F32)
+            return half[:, P * g : P * (g + 1)]
+
+        def turn_keys(c, b):
+            g, h = divmod(b, 2)
             bank = turn_psum.tile([P, 2, 2, P], F32, name="bank")
-            banks[c, g, h] = bank
+            banks[c, b] = bank
             for j in range(2):
                 for u in range(2):
-                    nc.tensor.transpose(bank[:, u, j, :], words(c, 2 * h + j, g, u), ident[:])
+                    nc.tensor.transpose(bank[:, u, j, :], key_pairs(c, 2 * h + j, g, u), ident[:])
 
-        def group(c, g, h):
-            if g == 0 and h == 0:
-                groups[c] = group_pool.tile([P, G, CH, 4], BF16, name="grp", align_bytes=64)
-            dst = groups[c][:, g, 256 * h : 256 * (h + 1), :].bitcast(F32)
-            nc.scalar.copy(out=dst, in_=banks[c, g, h][:].rearrange("p u j r -> p (j r) u"))
+        def empty_keys(c, b):
+            g, h = divmod(b, 2)
+            if b == 0:
+                turned[c] = turned_pool.tile([P, G, CHUNK, 4], BF16, name="turned_rows", align_bytes=64)
+            nc.scalar.copy(
+                out=turned[c][:, g, 2 * P * h : 2 * P * (h + 1), :].bitcast(F32),
+                in_=banks[c, b][:].rearrange("p u j r -> p (j r) u"),
+            )
 
-        def turn_q(m, h):
+        def turn_query(m, h):
             bank = turn_psum.tile([P, 2, 2, P], F32, name="bank")
-            banks["q", m, h] = bank
-            w = query_sb[:, m, :].bitcast(F32)
+            banks["query", m, h] = bank
             for j in range(2):
                 for u in range(2):
-                    g = 2 * h + j
-                    nc.tensor.transpose(bank[:, j, u, :], w[:, 256 * g + u : 256 * (g + 1) : 2], ident[:])
+                    nc.tensor.transpose(bank[:, j, u, :], natural_pairs(query_sb[:, m, :], 2 * h + j, u), ident[:])
 
-        def group_q(m, h):
+        def empty_query(m, h):
             if m == 0 and h == 0:
-                groups["q"] = group_pool.tile([P, G, CH, 4], BF16, name="grp", align_bytes=64)
-            dst = groups["q"][:, m, 256 * h : 256 * (h + 1), :].bitcast(F32).rearrange("p (j r) u -> p j r u", j=2)
-            nc.scalar.copy(out=dst, in_=banks["q", m, h][:].rearrange("p j u r -> p j r u"))
+                turned["query"] = turned_pool.tile([P, M, G * P, 4], BF16, name="turned_rows", align_bytes=64)
+            dst = turned["query"][:, m, 2 * P * h : 2 * P * (h + 1), :].bitcast(F32)
+            nc.scalar.copy(
+                out=dst.rearrange("p (j r) u -> p j r u", j=2),
+                in_=banks["query", m, h][:].rearrange("p j u r -> p j r u"),
+            )
 
-        def quant_q(m):
+
+        def quantize_keys(c, g):
+            if g == 0:
+                key_codes = code_pool.tile([P, G, CHUNK], U32, name="key_codes", align_bytes=64)
+                key_scales = code_pool.tile([P, G, CHUNK], U8, name="key_scales", align_bytes=64)
+                codes[c] = (key_codes, key_scales)
+            key_codes, key_scales = codes[c]
+            nc.vector.quantize_mx(
+                out=key_codes[:, g, :].bitcast(FP8X4),
+                scales=key_scales[:, g, :],
+                in_=turned[c][:, g].rearrange("p n t -> p (n t)"),
+            )
+
+        def quantize_query(m):
             nc.vector.quantize_mx(
                 out=q_codes[:, m].rearrange("p g r -> p (g r)").bitcast(FP8X4),
                 scales=q_scales[:, m].rearrange("p g r -> p (g r)"),
-                in_=groups["q"][:, m].rearrange("p n t -> p (n t)"))
+                in_=turned["query"][:, m].rearrange("p n t -> p (n t)"),
+            )
 
-        def quant(c, g):
-            if g == 0:
-                kc = code_pool.tile([P, G, CH], U32, name="kc", align_bytes=64)
-                ks = code_pool.tile([P, G, CH], U8, name="ks", align_bytes=64)
-                codes[c] = (kc, ks)
-            kc, ks = codes[c]
-            nc.vector.quantize_mx(
-                out=kc[:, g, :].bitcast(FP8X4), scales=ks[:, g, :], in_=groups[c][:, g].rearrange("p n t -> p (n t)"))
 
         def multiply(c, m):
-            kc, ks = codes[c]
-            acc = acc_psum.tile([P, CH], F32, name="acc")
-            accs[c, m] = acc
+            key_codes, key_scales = codes[c]
+            sums[c, m] = sum_psum.tile([P, CHUNK], F32, name="acc")
             for g in range(G):
                 nc.tensor.matmul_mx(
-                    out=acc[:], lhsT=q_codes[:, m, g, :].bitcast(FP8X4), lhsT_scale=q_scales[:, m, g, :],
-                    rhs=kc[:, g, :].bitcast(FP8X4), rhs_scale=ks[:, g, :],
-                    start=(g == 0), stop=(g == G - 1))
+                    out=sums[c, m][:],
+                    lhsT=q_codes[:, m, g, :].bitcast(FP8X4),
+                    lhsT_scale=q_scales[:, m, g, :],
+                    rhs=key_codes[:, g, :].bitcast(FP8X4),
+                    rhs_scale=key_scales[:, g, :],
+                    start=(g == 0),
+                    stop=(g == G - 1),
+                )
 
         def finish(c, m):
-            res = out_pool.tile([P, CH], F32, name="res")
+            cols = slice(CHUNK * c, CHUNK * (c + 1))
+            result = result_pool.tile([P, CHUNK], F32, name="scores")
             nc.vector.scalar_tensor_tensor(
-                out=res[:].rearrange("p (r i) -> p r i", i=NT),
-                in0=stale[:, CH * c : CH * (c + 1)].rearrange("p (r i) -> p r i", i=NT),
+                out=result[:].rearrange("p (r i) -> p r i", i=NT),
+                in0=stale[:, cols].rearrange("p (r i) -> p r i", i=NT),
                 scalar=neg_rate[:, m : m + 1],
-                in1=accs[c, m][:].rearrange("p (i r) -> p r i", i=NT),
-                op0=MULT, op1=ADD)
-            nc.sync.dma_start(out=out_view[:, m, CH * c : CH * (c + 1)], in_=res[:])
+                in1=sums[c, m][:].rearrange("p (i r) -> p r i", i=NT),
+                op0=MULT,
+                op1=ADD,
+            )
+            nc.sync.dma_start(out=out_view[:, m, cols], in_=result[:])
 
-        run = {"Ws": widen_s, "Wv": widen_v, "T": turn, "E": group, "Q": quant, "M": multiply, "O": finish,
-               "Tq": turn_q, "Eq": group_q, "Qq": quant_q}
+        def warm_up(n):
+            for i in range(n):
+                nc.tensor.matmul(idle_bank[:], lhsT=zeros[:, :P], rhs=zeros[:], start=True, stop=True)
 
-        def needs(op):
-            k, a = op[0], op[1:]
-            if k == "T":
-                return [(("Ws" if 4 * i + a[1] < 5 else "Wv"), a[0], i) for i in (2 * a[2], 2 * a[2] + 1)]
-            if k == "E":
-                return [("T",) + a]
-            if k == "Q":
-                return [("E",) + a + (h,) for h in range(2)]
-            if k == "M":
-                return [("Q", a[0], g) for g in range(G)] + [("Qq", a[1])]
-            if k == "O":
-                return [("M",) + a]
-            if k == "Eq":
-                return [("Tq",) + a]
-            if k == "Qq":
-                return [("Eq",) + a + (h,) for h in range(2)]
-            return []
-
-        def Ts(c):
-            return [("T", c, g, h) for g in range(G) for h in range(2)]
-
-        def Es(c):
-            return [("E", c, g, h) for g in range(G) for h in range(2)]
-
-        def Ms(c):
-            return [("M", c, m) for m in range(M)]
-
-        pe = Ts(0) + [("Tq", m, h) for m in range(M) for h in range(2)]
-        act = [("Ws", c, i) for c in (0, 1) for i in (0, 1)] + Es(0) + [("Eq", m, h) for m in range(M) for h in range(2)]
-        act += [("Ws", 2, 0), ("Ws", 2, 1)]
-        dve = [("Wv", c, i) for c in (0, 1) for i in (1, 2, 3)]
-        dve += [("Q", 0, 0), ("Q", 0, 1), ("Q", 0, 2), ("Wv", 2, 1), ("Q", 0, 3), ("Wv", 2, 2), ("Qq", 0), ("Qq", 1), ("Qq", 2), ("Wv", 2, 3), ("Qq", 3)]
-        for c in range(CHUNKS):
-            n, w = c + 1, c + 3
-            t, m = (Ts(n) if n < CHUNKS else []), Ms(c)
-            pe += t[:4] + m[:2] + t[4:] + m[2:]
-            act += [op for op in Es(n) + [("Ws", w, 0), ("Ws", w, 1)] if op[1] < CHUNKS]
-            dve += [op for op in [
-                ("O", c, 0), ("O", c, 1), ("Q", n, 0), ("Q", n, 1), ("Wv", w, 1),
-                ("O", c, 2), ("Q", n, 2), ("O", c, 3), ("Q", n, 3), ("Wv", w, 2), ("Wv", w, 3)] if op[1] < CHUNKS]
-
-        with tc.manual_schedule(engines=ENGINES):
-            nc.scalar.dma_start(out=key_scale0[:], in_=scale_view[:, 0, :])
+        with tc.manual_schedule():
+            nc.scalar.dma_start(out=scale_first[:], in_=scale_view[:, 0, :])
             nc.scalar.dma_start(out=age_sb[:], in_=age.rearrange("(p i) -> p i", p=P))
-            nc.scalar.dma_start(out=key_scale1[:], in_=scale_view[:, 1:, :])
+            nc.scalar.dma_start(out=scale_rest[:], in_=scale_view[:, 1:, :])
             nc.scalar.dma_start(out=rate_sb[:], in_=rate.rearrange("(p m) -> p m", m=M))
-            load(0, NT)
-            make_identity(nc, ident[:])
-            load(1, 2)
+            load_keys(0, parts=NT)
+            load_keys(1, parts=2)
             for m in range(M):
                 nc.sync.dma_start(out=query_sb[:, m, :], in_=query_view[:, m, :])
-            nc.scalar.activation(out=stale_sb[:], in_=age_sb[:], func=LN, bias=1.0)
-            nc.scalar.dma_start(out=park.rearrange("o (p i) -> p (o i)", p=P), in_=stale_sb[:])
-            nc.gpsimd.tensor_scalar(out=neg_rate[:], in0=rate_sb[:], scalar1=-1.0, scalar2=None, op0=MULT)
-            load(2, 2)
-            for c in range(CHUNKS):
-                nc.sync.dma_start(out=stale[:, CH * c : CH * (c + 1)],
-                                  in_=park[0, CH * c : CH * (c + 1)].partition_broadcast(P))
-                if c + 3 < CHUNKS:
-                    load(c + 3, 2)
 
-            queues = [pe, act, dve]
-            turns = [op for op in pe if op[0] in ("T", "Tq")]
-            mults = [op for op in pe if op[0] == "M"]
-            after = {}
-            for a, b in zip(turns, turns[6:]):
-                after[b] = ("E" + a[0][1:],) + a[1:]
-            for a, b in zip(mults, mults[2:]):
-                after[b] = ("O",) + a[1:]
-            for c in range(CHUNKS):
-                if c >= 4:
-                    after["Ws", c, 0] = after["Wv", c, 1] = ("T", c - 4, 3, 1)
-                if c >= 2:
-                    after["Q", c, 0] = ("M", c - 2, 3)
-                    after["E", c, 0, 0] = ("Qq", 3) if c == 2 else ("Q", c - 2, 3)
-            after["E", 1, 0, 0] = ("Q", 0, 3)
-            heads = [0, 0, 0]
-            done = set()
-            for lap in range(500):
-                for e in range(3):
-                    while heads[e] < len(queues[e]) and all(
-                        d in done for d in needs(queues[e][heads[e]]) + [after[op] for op in [queues[e][heads[e]]] if op in after]):
-                        op = queues[e][heads[e]]
-                        run[op[0]](*op[1:])
-                        done.add(op)
-                        heads[e] += 1
+            nc.vector.memset(zeros[:], 0.0)
+            make_identity(nc, ident[:])
+            nc.scalar.activation(out=stale_sb[:], in_=age_sb[:], func=LN, bias=1.0)
+            nc.gpsimd.tensor_scalar(out=neg_rate[:], in0=rate_sb[:], scalar1=-1.0, scalar2=None, op0=MULT)
+            nc.sync.dma_start(out=park.rearrange("o (p i) -> p (o i)", p=P), in_=stale_sb[:])
+            load_keys(2, parts=2)
+            for c in range(3, RAW_BUFS):
+                load_stale(c - 3)
+                load_keys(c, parts=2)
+            load_stale(RAW_BUFS - 3)
+
+            for c in range(2):
+                widen_scalar(c)
+                for i in range(1, NT):
+                    widen_vector(c, i)
+            idle_bank = sum_psum.tile([P, CHUNK], F32, name="acc")
+            warm_up(WARM_UP_HEAD)
+            for b in range(2 * G):
+                turn_keys(0, b)
+                warm_up(1)
+                empty_keys(0, b)
+            for m in range(M):
+                for h in range(2):
+                    turn_query(m, h)
+                    warm_up(1)
+                    empty_query(m, h)
+            widen_scalar(2)
+            for g in range(G):
+                quantize_keys(0, g)
+            widen_vector(2, 1)
+            quantize_query(0)
+            quantize_query(1)
+            widen_vector(2, 2)
+            quantize_query(2)
+            quantize_query(3)
+            widen_vector(2, 3)
+
+            for c in range(NC):
+                turning, widening, loading = c + 1 < NC, c + 3 < NC, c + RAW_BUFS < NC
+                if c + 3 < NC:
+                    load_stale(c + 3)
+                if loading:
+                    load_keys(c + RAW_BUFS, parts=2)
+                for half in range(2):
+                    if turning:
+                        for b in range(4 * half, 4 * half + 4):
+                            turn_keys(c + 1, b)
+                            empty_keys(c + 1, b)
+                    if turning and half == 1:
+                        quantize_keys(c + 1, 2)
+                    multiply(c, 2 * half)
+                    multiply(c, 2 * half + 1)
+                    finish(c, 2 * half)
+                    if turning and half == 1:
+                        quantize_keys(c + 1, 3)
+                    finish(c, 2 * half + 1)
+                    if turning and half == 0:
+                        quantize_keys(c + 1, 0)
+                        quantize_keys(c + 1, 1)
+                if widening:
+                    widen_scalar(c + 3)
+                    for i in range(1, NT):
+                        widen_vector(c + 3, i)

from contextlib import ExitStack

import concourse.mybir as mybir
from concourse.masks import make_identity

Q, T, K = 512, 4096, 2048
FLOPS = 2 * Q * T * K

F32 = mybir.dt.float32
BF16 = mybir.dt.bfloat16
U32 = mybir.dt.uint32
U8 = mybir.dt.uint8
FP8 = mybir.dt.float8_e4m3fn
FP8X4 = mybir.dt.float8_e4m3fn_x4
MULT = mybir.AluOpType.mult
ADD = mybir.AluOpType.add
COPY = mybir.ActivationFunctionType.Copy
LN = mybir.ActivationFunctionType.Ln

P = 128
PASS = 512
G = K // PASS
PAIRS = PASS // 2
CHUNK = 512
NT = CHUNK // P
NC = T // CHUNK
M = Q // P

SCALAR_WIDTHS = (K, PASS)

RAW_BUFS = 5
WIDE_BUFS = 4
TURN_BANKS = 5
SUM_BANKS = 3
WARM_UP_HEAD = 14


def tile_aged_key_retrieval_d3_kernel(tc, query, keys_bytes, keys_scale, age, rate, out):
    nc = tc.nc
    with ExitStack() as ctx:
        const = ctx.enter_context(tc.tile_pool(name="const", bufs=1))
        raw_pool = ctx.enter_context(tc.tile_pool(name="raw", bufs=RAW_BUFS))
        wide_pool = ctx.enter_context(tc.tile_pool(name="wide", bufs=WIDE_BUFS))
        turned_pool = ctx.enter_context(tc.tile_pool(name="turned", bufs=2))
        code_pool = ctx.enter_context(tc.tile_pool(name="code", bufs=2))
        result_pool = ctx.enter_context(tc.tile_pool(name="result", bufs=6))
        turn_psum = ctx.enter_context(tc.psum_pool(name="turn", bufs=TURN_BANKS))
        sum_psum = ctx.enter_context(tc.psum_pool(name="sum", bufs=SUM_BANKS))

        ident = const.tile([P, P], F32, name="ident")
        zeros = const.tile([P, CHUNK], BF16, name="zeros")
        scale_first = const.tile([P, NT], F32, name="scale_first")
        scale_rest = const.tile([P, NC - 1, NT], F32, name="scale_rest")
        age_sb = const.tile([P, T // P], BF16, name="age_sb")
        stale_sb = const.tile([P, T // P], F32, name="stale_sb")
        stale = const.tile([P, T], F32, name="stale")
        rate_sb = const.tile([P, M], BF16, name="rate_sb")
        neg_rate = const.tile([P, M], F32, name="neg_rate")
        query_sb = const.tile([P, M, K], BF16, name="query_sb")
        q_codes = const.tile([P, M, G, P], U32, name="q_codes", align_bytes=64)
        q_scales = const.tile([P, M, G, P], U8, name="q_scales", align_bytes=64)

        key_view = keys_bytes.rearrange("(c p i) k -> c p i k", p=P, i=NT)
        scale_view = keys_scale.rearrange("(c p i) o -> p c (i o)", p=P, i=NT)
        query_view = query.rearrange("(p m) k -> p m k", m=M)
        out_view = out.rearrange("(p m) n -> p m n", m=M)
        park = out[Q - 1 : Q, :]

        raw, natural, split, turned, codes, banks, sums = {}, {}, {}, {}, {}, {}, {}

        def load_keys(c, parts):
            raw[c] = raw_pool.tile([P, NT, K], U8, name="raw_keys")
            n = NT // parts
            for i in range(0, NT, n):
                nc.sync.dma_start(out=raw[c][:, i : i + n, :], in_=key_view[c][:, i : i + n, :])

        def load_stale(c):
            cols = slice(CHUNK * c, CHUNK * (c + 1))
            nc.sync.dma_start(out=stale[:, cols], in_=park[0, cols].partition_broadcast(P))

        def scale_col(c, i):
            return scale_first[:, i : i + 1] if c == 0 else scale_rest[:, c - 1, i : i + 1]


        def widen_scalar(c):
            natural[c] = wide_pool.tile([P, sum(SCALAR_WIDTHS)], BF16, name="natural")
            for i, width in enumerate(SCALAR_WIDTHS):
                nc.scalar.activation(
                    out=natural[c][:, K * i : K * i + width],
                    in_=raw[c][:, i, :width].bitcast(FP8),
                    func=COPY,
                    scale=scale_col(c, i),
                )

        def widen_vector(c, i):
            if i == 1:
                split[c] = wide_pool.tile([P, NT - 1, 2, K // 4, 2], BF16, name="split")
            k0 = SCALAR_WIDTHS[i] if i < len(SCALAR_WIDTHS) else 0
            nc.vector.tensor_scalar(
                out=split[c][:, i - 1, :, k0 // 4 :, :].rearrange("p u w e -> p w u e"),
                in0=raw[c][:, i, k0:].bitcast(FP8).rearrange("p (w u e) -> p w u e", u=2, e=2),
                scalar1=scale_col(c, i),
                scalar2=None,
                op0=MULT,
            )


        def natural_pairs(row, g, u):
            return row.bitcast(F32)[:, PAIRS * g + u : PAIRS * (g + 1) : 2]

        def key_pairs(c, i, g, u):
            if i < len(SCALAR_WIDTHS) and PASS * g < SCALAR_WIDTHS[i]:
                return natural_pairs(natural[c][:, K * i : K * i + SCALAR_WIDTHS[i]], g, u)
            half = split[c][:, i - 1, u].rearrange("p w e -> p (w e)").bitcast(F32)
            return half[:, P * g : P * (g + 1)]

        def turn_keys(c, b):
            g, h = divmod(b, 2)
            bank = turn_psum.tile([P, 2, 2, P], F32, name="bank")
            banks[c, b] = bank
            for j in range(2):
                for u in range(2):
                    nc.tensor.transpose(bank[:, u, j, :], key_pairs(c, 2 * h + j, g, u), ident[:])

        def empty_keys(c, b):
            g, h = divmod(b, 2)
            if b == 0:
                turned[c] = turned_pool.tile([P, G, CHUNK, 4], BF16, name="turned_rows", align_bytes=64)
            nc.scalar.copy(
                out=turned[c][:, g, 2 * P * h : 2 * P * (h + 1), :].bitcast(F32),
                in_=banks[c, b][:].rearrange("p u j r -> p (j r) u"),
            )

        def turn_query(m, h):
            bank = turn_psum.tile([P, 2, 2, P], F32, name="bank")
            banks["query", m, h] = bank
            for j in range(2):
                for u in range(2):
                    nc.tensor.transpose(bank[:, j, u, :], natural_pairs(query_sb[:, m, :], 2 * h + j, u), ident[:])

        def empty_query(m, h):
            if m == 0 and h == 0:
                turned["query"] = turned_pool.tile([P, M, G * P, 4], BF16, name="turned_rows", align_bytes=64)
            dst = turned["query"][:, m, 2 * P * h : 2 * P * (h + 1), :].bitcast(F32)
            nc.scalar.copy(
                out=dst.rearrange("p (j r) u -> p j r u", j=2),
                in_=banks["query", m, h][:].rearrange("p j u r -> p j r u"),
            )


        def quantize_keys(c, g):
            if g == 0:
                key_codes = code_pool.tile([P, G, CHUNK], U32, name="key_codes", align_bytes=64)
                key_scales = code_pool.tile([P, G, CHUNK], U8, name="key_scales", align_bytes=64)
                codes[c] = (key_codes, key_scales)
            key_codes, key_scales = codes[c]
            nc.vector.quantize_mx(
                out=key_codes[:, g, :].bitcast(FP8X4),
                scales=key_scales[:, g, :],
                in_=turned[c][:, g].rearrange("p n t -> p (n t)"),
            )

        def quantize_query(m):
            nc.vector.quantize_mx(
                out=q_codes[:, m].rearrange("p g r -> p (g r)").bitcast(FP8X4),
                scales=q_scales[:, m].rearrange("p g r -> p (g r)"),
                in_=turned["query"][:, m].rearrange("p n t -> p (n t)"),
            )


        def multiply(c, m):
            key_codes, key_scales = codes[c]
            sums[c, m] = sum_psum.tile([P, CHUNK], F32, name="acc")
            for g in range(G):
                nc.tensor.matmul_mx(
                    out=sums[c, m][:],
                    lhsT=q_codes[:, m, g, :].bitcast(FP8X4),
                    lhsT_scale=q_scales[:, m, g, :],
                    rhs=key_codes[:, g, :].bitcast(FP8X4),
                    rhs_scale=key_scales[:, g, :],
                    start=(g == 0),
                    stop=(g == G - 1),
                )

        def finish(c, m):
            cols = slice(CHUNK * c, CHUNK * (c + 1))
            result = result_pool.tile([P, CHUNK], F32, name="scores")
            nc.vector.scalar_tensor_tensor(
                out=result[:].rearrange("p (r i) -> p r i", i=NT),
                in0=stale[:, cols].rearrange("p (r i) -> p r i", i=NT),
                scalar=neg_rate[:, m : m + 1],
                in1=sums[c, m][:].rearrange("p (i r) -> p r i", i=NT),
                op0=MULT,
                op1=ADD,
            )
            nc.sync.dma_start(out=out_view[:, m, cols], in_=result[:])

        def warm_up(n):
            for i in range(n):
                nc.tensor.matmul(idle_bank[:], lhsT=zeros[:, :P], rhs=zeros[:], start=True, stop=True)

        with tc.manual_schedule():
            nc.scalar.dma_start(out=scale_first[:], in_=scale_view[:, 0, :])
            nc.scalar.dma_start(out=age_sb[:], in_=age.rearrange("(p i) -> p i", p=P))
            nc.scalar.dma_start(out=scale_rest[:], in_=scale_view[:, 1:, :])
            nc.scalar.dma_start(out=rate_sb[:], in_=rate.rearrange("(p m) -> p m", m=M))
            load_keys(0, parts=NT)
            load_keys(1, parts=2)
            for m in range(M):
                nc.sync.dma_start(out=query_sb[:, m, :], in_=query_view[:, m, :])

            nc.vector.memset(zeros[:], 0.0)
            make_identity(nc, ident[:])
            nc.scalar.activation(out=stale_sb[:], in_=age_sb[:], func=LN, bias=1.0)
            nc.gpsimd.tensor_scalar(out=neg_rate[:], in0=rate_sb[:], scalar1=-1.0, scalar2=None, op0=MULT)
            nc.sync.dma_start(out=park.rearrange("o (p i) -> p (o i)", p=P), in_=stale_sb[:])
            load_keys(2, parts=2)
            for c in range(3, RAW_BUFS):
                load_stale(c - 3)
                load_keys(c, parts=2)
            load_stale(RAW_BUFS - 3)

            for c in range(2):
                widen_scalar(c)
                for i in range(1, NT):
                    widen_vector(c, i)
            idle_bank = sum_psum.tile([P, CHUNK], F32, name="acc")
            warm_up(WARM_UP_HEAD)
            for b in range(2 * G):
                turn_keys(0, b)
                warm_up(1)
                empty_keys(0, b)
            for m in range(M):
                for h in range(2):
                    turn_query(m, h)
                    warm_up(1)
                    empty_query(m, h)
            widen_scalar(2)
            for g in range(G):
                quantize_keys(0, g)
            widen_vector(2, 1)
            quantize_query(0)
            quantize_query(1)
            widen_vector(2, 2)
            quantize_query(2)
            quantize_query(3)
            widen_vector(2, 3)

            for c in range(NC):
                turning, widening, loading = c + 1 < NC, c + 3 < NC, c + RAW_BUFS < NC
                if c + 3 < NC:
                    load_stale(c + 3)
                if loading:
                    load_keys(c + RAW_BUFS, parts=2)
                for half in range(2):
                    if turning:
                        for b in range(4 * half, 4 * half + 4):
                            turn_keys(c + 1, b)
                            empty_keys(c + 1, b)
                    if turning and half == 1:
                        quantize_keys(c + 1, 2)
                    multiply(c, 2 * half)
                    multiply(c, 2 * half + 1)
                    finish(c, 2 * half)
                    if turning and half == 1:
                        quantize_keys(c + 1, 3)
                    finish(c, 2 * half + 1)
                    if turning and half == 0:
                        quantize_keys(c + 1, 0)
                        quantize_keys(c + 1, 1)
                if widening:
                    widen_scalar(c + 3)
                    for i in range(1, NT):
                        widen_vector(c + 3, i)
